import numpy as np
import ml_dtypes


def mxq(x, axis, fmt="e4m3"):
    dtype, down = {"e4m3": (ml_dtypes.float8_e4m3fn, 7), "e5m2": (ml_dtypes.float8_e5m2, 14)}[fmt]
    v = np.moveaxis(np.asarray(x, np.float32).astype(ml_dtypes.bfloat16).astype(np.float64), axis, -1)
    blocks = v.reshape(v.shape[:-1] + (-1, 32))
    amax = np.abs(blocks).max(-1, keepdims=True)
    byte = np.maximum(np.where(amax > 0, np.frexp(amax)[1] - 1 + 127, 0) - down, 1)
    scale = np.exp2(byte - 127.0)
    codes = (blocks / scale).astype(np.float32).astype(dtype).astype(np.float64)
    return np.moveaxis((codes * scale).reshape(v.shape), -1, axis)


WIDE = False


def mx_kscale(k):
    if not WIDE:
        return np.ones(k)
    levels = np.array([10, -10, 5, -5, 0])
    if k % 512:
        return np.exp2(np.random.permutation(np.resize(levels, k // 32))).repeat(32)
    a = np.empty((k // 512, 16))
    for p in range(k // 512):
        a[p, :8] = np.random.permutation(np.resize(levels, 8))
        for g in range(8):
            far = levels[np.abs(levels - a[p, g]) >= 10]
            a[p, g + 8] = far[np.random.randint(len(far))]
    return np.exp2(a.ravel()).repeat(32)


def f64(x):
    return np.asarray(x).astype(np.float64)


def striped(idx):
    return np.tile(np.asarray(idx).reshape(-1, 16).T, (8, 1)).astype(np.uint16)


def unstriped(offs):
    return offs[:16].T.reshape(-1).astype(np.int64)


E2M1 = np.array([0.0, 0.5, 1.0, 1.5, 2.0, 3.0, 4.0, 6.0, -0.0, -0.5, -1.0, -1.5, -2.0, -3.0, -4.0, -6.0])


def pack_weight(w, fmt):
    k, n = w.shape
    w = f64(np.asarray(w, np.float32).astype(ml_dtypes.bfloat16)).reshape(k // 32, 32, n)
    amax = np.abs(w).max(1)
    if fmt == "e4m3":
        byte = np.frexp(amax)[1] - 1 + 127 - 7
    else:
        mant, ex = np.frexp(amax / 6.0)
        byte = np.where(mant > 0.5, ex, ex - 1) + 127
    byte = np.clip(np.where(amax > 0, byte, 1), 1, 254)
    scaled = (w * np.exp2(127.0 - byte)[:, None, :]).reshape(k, n).astype(np.float32)
    by_word = np.ascontiguousarray(scaled.reshape(k // 512, 128, 4, n).transpose(0, 1, 3, 2))
    if fmt == "e4m3":
        words = by_word.astype(ml_dtypes.float8_e4m3fn).view(np.uint8)
    else:
        c = by_word.astype(ml_dtypes.float4_e2m1fn).view(np.uint8) & 0xF
        words = (c[..., 0::2] | (c[..., 1::2] << 4)).reshape(k // 512, 128, 2 * n)
    return np.ascontiguousarray(words), np.ascontiguousarray(byte.astype(np.uint8).reshape(k // 512, 16, n))


def unpack_weight(words, scales, fmt):
    g, _, n = scales.shape
    words = np.ascontiguousarray(words).reshape(g, 128, n, -1)
    if fmt == "e4m3":
        vals = words.view(ml_dtypes.float8_e4m3fn).astype(np.float64)
    else:
        nib = np.empty((g, 128, n, 4), np.uint8)
        nib[..., 0::2] = words & 0xF
        nib[..., 1::2] = words >> 4
        vals = E2M1[nib]
    vals = vals * np.repeat(np.exp2(scales.astype(np.float64) - 127.0), 8, axis=1)[..., None]
    return vals.transpose(0, 1, 3, 2).reshape(g * 512, n)


B, N, T, D, DV, NQ = 2, 1536, 4096, 512, 128, 256
PAGE = 512


def setup_inputs():
    n = np.random.standard_normal
    pages = np.random.permutation(T // PAGE)[:B * N // PAGE]
    idx = (pages[:, None] * PAGE + np.arange(PAGE)[None, :]).reshape(-1)
    s = mx_kscale(D)[:, None]
    u = np.ones(T)
    u[idx] = mx_kscale(B * N)
    r = np.random.uniform(0.5, 2.0, T)
    k = n((D, T)) / s
    v = n((DV, T)) / (u * r)
    kp = pack_weight(k, "e4m3")
    vp = pack_weight(v.T, "e4m3")
    return {
        "qT": (n((B, D, NQ)) * s * (1.00 / np.sqrt(D))).astype(np.float32),
        "k_words": kp[0],
        "k_scales": kp[1],
        "v_words": vp[0],
        "v_scales": vp[1],
        "vs": np.tile(u * r, (128, 1)).astype(np.float32),
        "offs": striped(idx),
        "voffs": striped((pages[:, None] * DV + np.arange(DV)[None, :]).reshape(-1)),
    }


def reference(qT, k_words, k_scales, v_words, v_scales, vs, offs, voffs):
    idx = unstriped(offs)
    k = unpack_weight(k_words, k_scales, "e4m3")
    v = unpack_weight(v_words, v_scales, "e4m3")
    v = v.reshape(T // 512, 512, DV)[unstriped(voffs)[::DV] // DV].reshape(B, N, DV)
    pick = lambda x: x[:, idx].reshape(x.shape[0], B, N).transpose(1, 0, 2)
    q = f64(qT)
    score = mxq(q, 1, "e4m3").transpose(0, 2, 1) @ pick(k)
    m = score.max(-1, keepdims=True)
    p = np.exp(score - m)
    total = p.sum(-1, keepdims=True)
    w = p * pick(f64(vs))[:, :1, :]
    y = mxq(w, 2, "e4m3") @ v
    y = y / total
    return y

@@ -1,0 +1,204 @@
+from contextlib import ExitStack
+
+import concourse.mybir as mybir
+from concourse.masks import make_identity
+
+B, N, T, D, DV, NQ = 2, 1536, 4096, 512, 128, 256
+PAGE = 512
+FLOPS = 2 * B * NQ * N * (D + DV)
+
+F32 = mybir.dt.float32
+BF16 = mybir.dt.bfloat16
+I32 = mybir.dt.int32
+U32 = mybir.dt.uint32
+U16 = mybir.dt.uint16
+U8 = mybir.dt.uint8
+FP8X4 = mybir.dt.float8_e4m3fn_x4
+ACT = mybir.ActivationFunctionType
+ALU = mybir.AluOpType
+AX = mybir.AxisListType
+
+P = 128
+PACK = 4
+PAGES = N // PAGE
+QT = NQ // P
+LIST_COLS = PAGE // 16
+VLIST_COLS = DV // 16
+
+
+def tile_attend_pkv8_soft_kernel(tc, qT, k_words, k_scales, v_words, v_scales, vs, offs, voffs, out):
+    nc = tc.nc
+    with ExitStack() as ctx:
+        lists = ctx.enter_context(tc.tile_pool(name="lists", bufs=1))
+        keep = ctx.enter_context(tc.tile_pool(name="keep", bufs=1))
+        ring = ctx.enter_context(tc.tile_pool(name="ring", bufs=3))
+        slots = ctx.enter_context(tc.tile_pool(name="slots", bufs=1))
+        ps_page = ctx.enter_context(tc.psum_pool(name="ps_page", bufs=1))
+        ps_out = ctx.enter_context(tc.psum_pool(name="ps_out", bufs=2))
+
+        offs_sb = lists.tile([P, B * N // 16], U16, name="offs_sb")
+        voffs_sb = lists.tile([P, B * PAGES * DV // 16], U16, name="voffs_sb")
+
+        kw_pool = keep.tile([P, T], I32, name="kw_pool", align_bytes=64)
+        ks_pool = keep.tile([P, T], U8, name="ks_pool", align_bytes=64)
+        vw_pool = keep.tile([P, T // PAGE * DV], I32, name="vw_pool", align_bytes=64)
+        vsc_pool = keep.tile([P, T // PAGE * DV], U8, name="vsc_pool", align_bytes=64)
+        ts_pool = keep.tile([P, T], F32, name="ts_pool", align_bytes=64)
+        ident = keep.tile([P, P], F32, name="ident", align_bytes=64)
+        warm = keep.tile([P, 8], F32, name="warm")
+        warm_out = keep.tile([P, 8], F32, name="warm_out")
+
+        nc.vector.memset(ks_pool[:].bitcast(I32), 0)
+        nc.vector.memset(warm[:], 0.0)
+        nc.scalar.activation(warm_out[:], warm[:], ACT.Exp)
+        nc.vector.memset(ts_pool[:], 0.0)
+        nc.vector.memset(vsc_pool[:].bitcast(I32), 0)
+        make_identity(nc, ident[:])
+
+        nc.sync.dma_start(offs_sb[:], offs)
+        for quad in range(4):
+            nc.sync.dma_start(ks_pool[32 * quad : 32 * quad + 4, :].bitcast(I32),
+                              k_scales[0, 4 * quad : 4 * quad + 4, :].bitcast(I32))
+        nc.sync.dma_start(kw_pool[:], k_words[0].rearrange("p n r -> p (n r)").bitcast(I32))
+        q_raw = []
+        for b in range(B):
+            q_raw.append(keep.tile([P, PACK, NQ], F32, name=f"q_raw{b}"))
+        nc.sync.dma_start(q_raw[0][:], qT[0].rearrange("(p j) q -> p j q", j=PACK))
+        nc.sync.dma_start(ts_pool[0:1, :], vs[0:1, :])
+        nc.sync.dma_start(q_raw[1][:], qT[1].rearrange("(p j) q -> p j q", j=PACK))
+        nc.sync.dma_start(voffs_sb[:], voffs)
+        nc.sync.dma_start(vw_pool[:].rearrange("p (u e) -> p u e", e=DV),
+                          v_words.rearrange("u p e r -> p u (e r)").bitcast(I32))
+        for quad in range(4):
+            nc.sync.dma_start(vsc_pool[32 * quad : 32 * quad + 4, :].bitcast(I32).rearrange("p (u e) -> p u e", u=T // PAGE),
+                              v_scales[:, 4 * quad : 4 * quad + 4, :].rearrange("u f e -> f u e").bitcast(I32))
+
+        kw, ks, tsc, qw, qs = {}, {}, {}, {}, {}
+        neg_max, sums, p_sb, ww, wsc, banks, inv, values = {}, {}, {}, {}, {}, {}, {}, {}
+
+        def page_list(b, e, pages=1):
+            c0 = (b * PAGES + e) * LIST_COLS
+            return offs_sb[:, c0 : c0 + pages * LIST_COLS]
+
+        def gather_key_scales(b, e, tag):
+            ks[b, e] = slots.tile([P, PAGE], U8, name=f"ks{b}_{e}", tag=tag, align_bytes=64)
+            nc.vector.tensor_copy(ks[b, e][:], ks_pool[:].indirect(page_list(b, e)))
+
+        def gather_key_words(b, e):
+            kw[b, e] = slots.tile([P, PAGE], U32, name=f"kw{b}_{e}", tag=f"kw{e}", align_bytes=64)
+            nc.vector.tensor_copy(kw[b, e][:], kw_pool[:].bitcast(U32).indirect(page_list(b, e)))
+
+        def gather_token_scales(b, e0, pages, tag):
+            row = slots.tile([P, pages * PAGE], F32, name=f"ts_row{b}_{e0}", tag=tag, align_bytes=64)
+            nc.vector.tensor_copy(row[:], ts_pool[:].indirect(page_list(b, e0, pages)))
+            for i in range(pages):
+                tsc[b, e0 + i] = keep.tile([P, PACK], F32, name=f"tsc{b}_{e0 + i}")
+                nc.sync.dma_start(tsc[b, e0 + i][:],
+                                  row[0:1, i * PAGE : (i + 1) * PAGE].rearrange("o (s t) -> o s t", t=PACK))
+
+        def gather_values():
+            values["words"] = keep.tile([P, B * PAGES * DV], U32, name="vw", align_bytes=64)
+            values["scales"] = keep.tile([P, B * PAGES * DV], U8, name="vsc", align_bytes=64)
+            nc.vector.tensor_copy(values["words"][:], vw_pool[:].bitcast(U32).indirect(voffs_sb[:]))
+            nc.vector.tensor_copy(values["scales"][:], vsc_pool[:].indirect(voffs_sb[:]))
+
+        def quantise_queries(b, h, tag):
+            grouped = slots.tile([P, P, PACK], BF16, name=f"q_grouped{b}_{h}", tag=tag, align_bytes=64)
+            nc.scalar.copy(grouped[:], q_raw[b][:, :, h * P : (h + 1) * P].rearrange("p j q -> p q j"))
+            qw[b, h] = keep.tile([P, P], U32, name=f"qw{b}_{h}", align_bytes=64)
+            qs[b, h] = keep.tile([P, P], U8, name=f"qs{b}_{h}", align_bytes=64)
+            nc.vector.quantize_mx(out=qw[b, h][:].bitcast(FP8X4), scales=qs[b, h][:],
+                                  in_=grouped[:].rearrange("p q j -> p (q j)"))
+
+        def scores(b, h):
+            page_max = slots.tile([P, PAGES], F32, name=f"page_max{b}_{h}", tag=f"max{b}_{h}", align_bytes=64)
+            for e in range(PAGES):
+                bank = ps_page.tile([P, PAGE], F32, name=f"score{b}_{h}_{e}", tag=f"bank{h}_{e}")
+                banks[b, h, e] = bank
+                nc.tensor.matmul_mx(out=bank[:], lhsT=qw[b, h][:].bitcast(FP8X4), lhsT_scale=qs[b, h][:],
+                                    rhs=kw[b, e][:].bitcast(FP8X4), rhs_scale=ks[b, e][:],
+                                    start=True, stop=True)
+                nc.vector.tensor_reduce(page_max[:, e : e + 1], bank[:], AX.X, ALU.max)
+            neg_max[b, h] = keep.tile([P, 1], F32, name=f"neg_max{b}_{h}")
+            nc.vector.tensor_reduce(neg_max[b, h][:], page_max[:], AX.X, ALU.max, negate=True)
+
+        def exps(b, h):
+            if h == 0:
+                sums[b] = keep.tile([P, QT, PAGES], F32, name=f"sums{b}")
+            for e in range(PAGES):
+                p_sb[b, h, e] = keep.tile([P, PACK, P], F32, name=f"p{b}_{h}_{e}", align_bytes=64)
+                nc.scalar.activation(p_sb[b, h, e][:], banks[b, h, e][:].rearrange("q (s t) -> q t s", t=PACK),
+                                     ACT.Exp, bias=neg_max[b, h][:], accum_out=sums[b][:, h, e : e + 1])
+
+        def row_sums(b):
+            total = keep.tile([P, QT], F32, name=f"total{b}")
+            nc.vector.tensor_reduce(total[:], sums[b][:], AX.X, ALU.add)
+            inv[b] = keep.tile([P, QT], F32, name=f"inv{b}")
+            nc.vector.reciprocal(inv[b][:], total[:])
+
+        def weights(b, h, e, on_vector):
+            turned = ps_page.tile([P, PACK, P], F32, name=f"turned{b}_{h}_{e}", tag=f"bank{h}_{e}")
+            for t in range(PACK):
+                nc.tensor.transpose(turned[:, t, :], p_sb[b, h, e][:, t, :], ident[:])
+            woven = keep.tile([P, P, PACK], BF16, name=f"woven{b}_{h}_{e}", align_bytes=64)
+            if on_vector:
+                nc.vector.tensor_tensor(woven[:], turned[:].rearrange("s t q -> s q t"),
+                                        tsc[b, e][:].unsqueeze(1).to_broadcast([P, P, PACK]), ALU.mult)
+            else:
+                planes = ring.tile([P, PACK, P], BF16, name="planes", align_bytes=64)
+                for t in range(PACK):
+                    nc.scalar.activation(planes[:, t, :], turned[:, t, :], ACT.Copy, scale=tsc[b, e][:, t : t + 1])
+                nc.scalar.copy(woven[:], planes[:].rearrange("s t q -> s q t"))
+            ww[b, h, e] = keep.tile([P, P], U32, name=f"ww{b}_{h}_{e}", align_bytes=64)
+            wsc[b, h, e] = keep.tile([P, P], U8, name=f"wsc{b}_{h}_{e}", align_bytes=64)
+            nc.vector.quantize_mx(out=ww[b, h, e][:].bitcast(FP8X4), scales=wsc[b, h, e][:],
+                                  in_=woven[:].rearrange("s q t -> s (q t)"))
+
+        def finish(b, h):
+            acc = ps_out.tile([P, DV], F32, name="acc")
+            for e in range(PAGES):
+                cols = slice((b * PAGES + e) * DV, (b * PAGES + e + 1) * DV)
+                nc.tensor.matmul_mx(out=acc[:], lhsT=ww[b, h, e][:].bitcast(FP8X4), lhsT_scale=wsc[b, h, e][:],
+                                    rhs=values["words"][:, cols].bitcast(FP8X4), rhs_scale=values["scales"][:, cols],
+                                    start=(e == 0), stop=(e == PAGES - 1))
+            y = keep.tile([P, DV], F32, name=f"y{b}_{h}")
+            nc.scalar.activation(y[:], acc[:], ACT.Copy, scale=inv[b][:, h : h + 1])
+            nc.sync.dma_start(out[b, h * P : (h + 1) * P, :], y[:])
+
+        for e in range(PAGES):
+            gather_key_scales(0, e, f"ks{e}")
+        gather_key_scales(1, 0, "ks_early")
+        gather_key_words(0, 0)
+        gather_key_words(0, 1)
+        quantise_queries(0, 0, "kw2")
+        gather_key_words(0, 2)
+        quantise_queries(0, 1, "row_a")
+        gather_token_scales(0, 0, 1, "row_a")
+        scores(0, 0)
+        scores(0, 1)
+        exps(0, 0)
+        exps(0, 1)
+        gather_token_scales(0, 1, 2, "max0_1")
+        quantise_queries(1, 0, "q10")
+        quantise_queries(1, 1, "q11")
+        for e in range(PAGES):
+            if e > 0:
+                gather_key_scales(1, e, f"ks{e}")
+            gather_key_words(1, e)
+        gather_token_scales(1, 0, 3, "row_a")
+        gather_values()
+        row_sums(0)
+        for h in range(QT):
+            for e in range(PAGES):
+                weights(0, h, e, False)
+        scores(1, 0)
+        exps(1, 0)
+        finish(0, 0)
+        scores(1, 1)
+        exps(1, 1)
+        finish(0, 1)
+        row_sums(1)
+        for h in range(QT):
+            for e in range(PAGES):
+                weights(1, h, e, (h, e) != (0, 2))
+            finish(1, h)

@@ -23,7 +23,8 @@ PACK = 4
 PAGES = N // PAGE
 QT = NQ // P
 LIST_COLS = PAGE // 16
-VLIST_COLS = DV // 16
+TS_ROW = 80
+SCORE_BANK = {(b, h, e): f"bank{PAGES * h + e}" for b in range(B) for h in range(QT) for e in range(PAGES)}
 
 
 def tile_attend_pkv8_soft_kernel(tc, qT, k_words, k_scales, v_words, v_scales, vs, offs, voffs, out):
@@ -34,15 +35,11 @@ def tile_attend_pkv8_soft_kernel(tc, qT, k_words, k_scales, v_words, v_scales, v
         ring = ctx.enter_context(tc.tile_pool(name="ring", bufs=3))
         slots = ctx.enter_context(tc.tile_pool(name="slots", bufs=1))
         ps_page = ctx.enter_context(tc.psum_pool(name="ps_page", bufs=1))
-        ps_out = ctx.enter_context(tc.psum_pool(name="ps_out", bufs=2))
 
         offs_sb = lists.tile([P, B * N // 16], U16, name="offs_sb")
         voffs_sb = lists.tile([P, B * PAGES * DV // 16], U16, name="voffs_sb")
 
-        kw_pool = keep.tile([P, T], I32, name="kw_pool", align_bytes=64)
         ks_pool = keep.tile([P, T], U8, name="ks_pool", align_bytes=64)
-        vw_pool = keep.tile([P, T // PAGE * DV], I32, name="vw_pool", align_bytes=64)
-        vsc_pool = keep.tile([P, T // PAGE * DV], U8, name="vsc_pool", align_bytes=64)
         ts_pool = keep.tile([P, T], F32, name="ts_pool", align_bytes=64)
         ident = keep.tile([P, P], F32, name="ident", align_bytes=64)
         warm = keep.tile([P, 8], F32, name="warm")
@@ -52,26 +49,27 @@ def tile_attend_pkv8_soft_kernel(tc, qT, k_words, k_scales, v_words, v_scales, v
         nc.vector.memset(warm[:], 0.0)
         nc.scalar.activation(warm_out[:], warm[:], ACT.Exp)
         nc.vector.memset(ts_pool[:], 0.0)
-        nc.vector.memset(vsc_pool[:].bitcast(I32), 0)
-        make_identity(nc, ident[:])
+        nc.vector.memset(ident[:], 0.0)
+        make_identity(nc, ident[:], nomemset=True)
 
+        q_raw = {}
+
+        def load_queries(b, h0, tiles, tag):
+            raw = slots.tile([P, PACK, tiles * P], F32, name=f"q_raw{b}_{h0}", tag=tag, align_bytes=64)
+            nc.sync.dma_start(raw[:], qT[b][:, h0 * P : (h0 + tiles) * P].rearrange("(p j) q -> p j q", j=PACK))
+            for i in range(tiles):
+                q_raw[b, h0 + i] = raw[:, :, i * P : (i + 1) * P]
+
+        load_queries(0, 0, 1, "q_first")
         nc.sync.dma_start(offs_sb[:], offs)
-        for quad in range(4):
-            nc.sync.dma_start(ks_pool[32 * quad : 32 * quad + 4, :].bitcast(I32),
-                              k_scales[0, 4 * quad : 4 * quad + 4, :].bitcast(I32))
-        nc.sync.dma_start(kw_pool[:], k_words[0].rearrange("p n r -> p (n r)").bitcast(I32))
-        q_raw = []
-        for b in range(B):
-            q_raw.append(keep.tile([P, PACK, NQ], F32, name=f"q_raw{b}"))
-        nc.sync.dma_start(q_raw[0][:], qT[0].rearrange("(p j) q -> p j q", j=PACK))
-        nc.sync.dma_start(ts_pool[0:1, :], vs[0:1, :])
-        nc.sync.dma_start(q_raw[1][:], qT[1].rearrange("(p j) q -> p j q", j=PACK))
         nc.sync.dma_start(voffs_sb[:], voffs)
-        nc.sync.dma_start(vw_pool[:].rearrange("p (u e) -> p u e", e=DV),
-                          v_words.rearrange("u p e r -> p u (e r)").bitcast(I32))
-        for quad in range(4):
-            nc.sync.dma_start(vsc_pool[32 * quad : 32 * quad + 4, :].bitcast(I32).rearrange("p (u e) -> p u e", u=T // PAGE),
-                              v_scales[:, 4 * quad : 4 * quad + 4, :].rearrange("u f e -> f u e").bitcast(I32))
+        for r in range(4):
+            nc.sync.dma_start(ks_pool[r:P:32, :].bitcast(I32), k_scales[0, r:16:4, :].bitcast(I32))
+        kw_pool = keep.tile([P, T], I32, name="kw_pool", align_bytes=64)
+        nc.sync.dma_start(kw_pool[:], k_words[0].rearrange("p n r -> p (n r)").bitcast(I32))
+        load_queries(0, 1, 1, "q_second")
+        load_queries(1, 0, 2, "q_third")
+        nc.scalar.dma_start(ts_pool[TS_ROW : TS_ROW + 1, :], vs[TS_ROW : TS_ROW + 1, :])
 
         kw, ks, tsc, qw, qs = {}, {}, {}, {}, {}
         neg_max, sums, p_sb, ww, wsc, banks, inv, values = {}, {}, {}, {}, {}, {}, {}, {}
@@ -80,9 +78,9 @@ def tile_attend_pkv8_soft_kernel(tc, qT, k_words, k_scales, v_words, v_scales, v
             c0 = (b * PAGES + e) * LIST_COLS
             return offs_sb[:, c0 : c0 + pages * LIST_COLS]
 
-        def gather_key_scales(b, e, tag):
-            ks[b, e] = slots.tile([P, PAGE], U8, name=f"ks{b}_{e}", tag=tag, align_bytes=64)
-            nc.vector.tensor_copy(ks[b, e][:], ks_pool[:].indirect(page_list(b, e)))
+        def gather_key_scales(b):
+            ks[b] = keep.tile([P, N], U8, name=f"ks{b}", align_bytes=64)
+            nc.vector.tensor_copy(ks[b][:], ks_pool[:].indirect(page_list(b, 0, PAGES)))
 
         def gather_key_words(b, e):
             kw[b, e] = slots.tile([P, PAGE], U32, name=f"kw{b}_{e}", tag=f"kw{e}", align_bytes=64)
@@ -94,18 +92,30 @@ def tile_attend_pkv8_soft_kernel(tc, qT, k_words, k_scales, v_words, v_scales, v
             for i in range(pages):
                 tsc[b, e0 + i] = keep.tile([P, PACK], F32, name=f"tsc{b}_{e0 + i}")
                 nc.sync.dma_start(tsc[b, e0 + i][:],
-                                  row[0:1, i * PAGE : (i + 1) * PAGE].rearrange("o (s t) -> o s t", t=PACK))
+                                  row[TS_ROW : TS_ROW + 1, i * PAGE : (i + 1) * PAGE].rearrange("o (s t) -> o s t", t=PACK))
+
+        def load_values():
+            vw_pool = slots.tile([P, T // PAGE * DV], I32, name="vw_pool", tag="q10", align_bytes=64)
+            vsc_pool = slots.tile([P, T // PAGE * DV], U8, name="vsc_pool", tag="q11", align_bytes=64)
+            nc.sync.dma_start(vw_pool[:].rearrange("p (u e) -> p u e", e=DV),
+                              v_words.rearrange("u p e r -> p u (e r)").bitcast(I32))
+            nc.vector.memset(vsc_pool[:].bitcast(I32), 0)
+            for r in range(4):
+                rows = vsc_pool[r:P:32, :].bitcast(I32)
+                nc.sync.dma_start(rows.rearrange("p (u e) -> p u e", u=T // PAGE),
+                                  v_scales[:, r:16:4, :].rearrange("u f e -> f u e").bitcast(I32))
+            values["word_pool"], values["scale_pool"] = vw_pool, vsc_pool
 
         def gather_values():
-            values["words"] = keep.tile([P, B * PAGES * DV], U32, name="vw", align_bytes=64)
-            values["scales"] = keep.tile([P, B * PAGES * DV], U8, name="vsc", align_bytes=64)
-            nc.vector.tensor_copy(values["words"][:], vw_pool[:].bitcast(U32).indirect(voffs_sb[:]))
-            nc.vector.tensor_copy(values["scales"][:], vsc_pool[:].indirect(voffs_sb[:]))
+            values["words"] = slots.tile([P, B * PAGES * DV], U32, name="vw", tag="vwown", align_bytes=64)
+            nc.vector.tensor_copy(values["words"][:], values["word_pool"][:].bitcast(U32).indirect(voffs_sb[:]))
+            values["scales"] = slots.tile([P, B * PAGES * DV], U8, name="vsc", tag="q10", align_bytes=64)
+            nc.vector.tensor_copy(values["scales"][:], values["scale_pool"][:].indirect(voffs_sb[:]))
 
         def quantise_queries(b, h, tag):
             grouped = slots.tile([P, P, PACK], BF16, name=f"q_grouped{b}_{h}", tag=tag, align_bytes=64)
-            nc.scalar.copy(grouped[:], q_raw[b][:, :, h * P : (h + 1) * P].rearrange("p j q -> p q j"))
-            qw[b, h] = keep.tile([P, P], U32, name=f"qw{b}_{h}", align_bytes=64)
+            nc.scalar.copy(grouped[:], q_raw[b, h].rearrange("p j q -> p q j"))
+            qw[b, h] = slots.tile([P, P], U32, name=f"qw{b}_{h}", tag=f"qw{b}{h}", align_bytes=64)
             qs[b, h] = keep.tile([P, P], U8, name=f"qs{b}_{h}", align_bytes=64)
             nc.vector.quantize_mx(out=qw[b, h][:].bitcast(FP8X4), scales=qs[b, h][:],
                                   in_=grouped[:].rearrange("p q j -> p (q j)"))
@@ -113,20 +123,21 @@ def tile_attend_pkv8_soft_kernel(tc, qT, k_words, k_scales, v_words, v_scales, v
         def scores(b, h):
             page_max = slots.tile([P, PAGES], F32, name=f"page_max{b}_{h}", tag=f"max{b}_{h}", align_bytes=64)
             for e in range(PAGES):
-                bank = ps_page.tile([P, PAGE], F32, name=f"score{b}_{h}_{e}", tag=f"bank{h}_{e}")
+                bank = ps_page.tile([P, PAGE], F32, name=f"score{b}_{h}_{e}", tag=SCORE_BANK[b, h, e])
                 banks[b, h, e] = bank
                 nc.tensor.matmul_mx(out=bank[:], lhsT=qw[b, h][:].bitcast(FP8X4), lhsT_scale=qs[b, h][:],
-                                    rhs=kw[b, e][:].bitcast(FP8X4), rhs_scale=ks[b, e][:],
+                                    rhs=kw[b, e][:].bitcast(FP8X4), rhs_scale=ks[b][:, e * PAGE : (e + 1) * PAGE],
                                     start=True, stop=True)
                 nc.vector.tensor_reduce(page_max[:, e : e + 1], bank[:], AX.X, ALU.max)
             neg_max[b, h] = keep.tile([P, 1], F32, name=f"neg_max{b}_{h}")
             nc.vector.tensor_reduce(neg_max[b, h][:], page_max[:], AX.X, ALU.max, negate=True)
 
-        def exps(b, h):
+        def exps(b, h, first_tag):
             if h == 0:
                 sums[b] = keep.tile([P, QT, PAGES], F32, name=f"sums{b}")
             for e in range(PAGES):
-                p_sb[b, h, e] = keep.tile([P, PACK, P], F32, name=f"p{b}_{h}_{e}", align_bytes=64)
+                p_sb[b, h, e] = slots.tile([P, PACK, P], F32, name=f"p{b}_{h}_{e}", align_bytes=64,
+                                           tag=first_tag if e == 0 else f"p{b}_{h}_{e}")
                 nc.scalar.activation(p_sb[b, h, e][:], banks[b, h, e][:].rearrange("q (s t) -> q t s", t=PACK),
                                      ACT.Exp, bias=neg_max[b, h][:], accum_out=sums[b][:, h, e : e + 1])
 
@@ -136,8 +147,30 @@ def tile_attend_pkv8_soft_kernel(tc, qT, k_words, k_scales, v_words, v_scales, v
             inv[b] = keep.tile([P, QT], F32, name=f"inv{b}")
             nc.vector.reciprocal(inv[b][:], total[:])
 
+        def weave(woven, planes):
+            nc.scalar.copy(woven[:].rearrange("s (c i) t -> s c t i", i=4), planes[:].rearrange("s t (c i) -> s c t i", i=4))
+
+        def weights_pair(b, e):
+            planes = slots.tile([P, PACK, NQ], BF16, name=f"planes2_{e}", tag=f"planes{e}", align_bytes=64)
+            for half in range(2):
+                turned = ps_page.tile([P, 2, NQ], F32, name=f"turned{b}_{half}_{e}", tag=f"bank{6 + half}")
+                for i in range(2):
+                    for h in range(QT):
+                        nc.tensor.transpose(turned[:, i, h * P : (h + 1) * P], p_sb[b, h, e][:, 2 * half + i, :], ident[:])
+                for i in range(2):
+                    t = 2 * half + i
+                    nc.scalar.activation(planes[:, t, :], turned[:, i, :], ACT.Copy, scale=tsc[b, e][:, t : t + 1])
+            woven = keep.tile([P, NQ, PACK], BF16, name=f"woven{b}_{e}", align_bytes=64)
+            weave(woven, planes)
+            words = keep.tile([P, NQ], U32, name=f"ww{b}_{e}", align_bytes=64)
+            scales = keep.tile([P, NQ], U8, name=f"wsc{b}_{e}", align_bytes=64)
+            nc.vector.quantize_mx(out=words[:].bitcast(FP8X4), scales=scales[:], in_=woven[:].rearrange("s q t -> s (q t)"))
+            for h in range(QT):
+                ww[b, h, e] = words[:, h * P : (h + 1) * P]
+                wsc[b, h, e] = scales[:, h * P : (h + 1) * P]
+
         def weights(b, h, e, on_vector):
-            turned = ps_page.tile([P, PACK, P], F32, name=f"turned{b}_{h}_{e}", tag=f"bank{h}_{e}")
+            turned = ps_page.tile([P, PACK, P], F32, name=f"turned{b}_{h}_{e}", tag=SCORE_BANK[b, h, e])
             for t in range(PACK):
                 nc.tensor.transpose(turned[:, t, :], p_sb[b, h, e][:, t, :], ident[:])
             woven = keep.tile([P, P, PACK], BF16, name=f"woven{b}_{h}_{e}", align_bytes=64)
@@ -148,57 +181,54 @@ def tile_attend_pkv8_soft_kernel(tc, qT, k_words, k_scales, v_words, v_scales, v
                 planes = ring.tile([P, PACK, P], BF16, name="planes", align_bytes=64)
                 for t in range(PACK):
                     nc.scalar.activation(planes[:, t, :], turned[:, t, :], ACT.Copy, scale=tsc[b, e][:, t : t + 1])
-                nc.scalar.copy(woven[:], planes[:].rearrange("s t q -> s q t"))
-            ww[b, h, e] = keep.tile([P, P], U32, name=f"ww{b}_{h}_{e}", align_bytes=64)
-            wsc[b, h, e] = keep.tile([P, P], U8, name=f"wsc{b}_{h}_{e}", align_bytes=64)
-            nc.vector.quantize_mx(out=ww[b, h, e][:].bitcast(FP8X4), scales=wsc[b, h, e][:],
-                                  in_=woven[:].rearrange("s q t -> s (q t)"))
+                weave(woven, planes)
+            words = keep.tile([P, P], U32, name=f"ww{b}_{h}_{e}", align_bytes=64)
+            scales = keep.tile([P, P], U8, name=f"wsc{b}_{h}_{e}", align_bytes=64)
+            nc.vector.quantize_mx(out=words[:].bitcast(FP8X4), scales=scales[:], in_=woven[:].rearrange("s q t -> s (q t)"))
+            ww[b, h, e], wsc[b, h, e] = words[:], scales[:]
 
-        def finish(b, h):
-            acc = ps_out.tile([P, DV], F32, name="acc")
+        def finish(b, h, tag):
+            acc = ps_page.tile([P, DV], F32, name=f"acc{b}_{h}", tag=tag)
             for e in range(PAGES):
                 cols = slice((b * PAGES + e) * DV, (b * PAGES + e + 1) * DV)
-                nc.tensor.matmul_mx(out=acc[:], lhsT=ww[b, h, e][:].bitcast(FP8X4), lhsT_scale=wsc[b, h, e][:],
+                nc.tensor.matmul_mx(out=acc[:], lhsT=ww[b, h, e].bitcast(FP8X4), lhsT_scale=wsc[b, h, e],
                                     rhs=values["words"][:, cols].bitcast(FP8X4), rhs_scale=values["scales"][:, cols],
                                     start=(e == 0), stop=(e == PAGES - 1))
             y = keep.tile([P, DV], F32, name=f"y{b}_{h}")
             nc.scalar.activation(y[:], acc[:], ACT.Copy, scale=inv[b][:, h : h + 1])
             nc.sync.dma_start(out[b, h * P : (h + 1) * P, :], y[:])
 
+        quantise_queries(0, 0, "q00")
+        gather_key_scales(0)
+        gather_key_scales(1)
         for e in range(PAGES):
-            gather_key_scales(0, e, f"ks{e}")
-        gather_key_scales(1, 0, "ks_early")
-        gather_key_words(0, 0)
-        gather_key_words(0, 1)
-        quantise_queries(0, 0, "kw2")
-        gather_key_words(0, 2)
+            gather_key_words(0, e)
+        scores(0, 0)
         quantise_queries(0, 1, "row_a")
         gather_token_scales(0, 0, 1, "row_a")
-        scores(0, 0)
         scores(0, 1)
-        exps(0, 0)
-        exps(0, 1)
-        gather_token_scales(0, 1, 2, "max0_1")
+        exps(0, 0, "p00")
+        exps(0, 1, "p01")
         quantise_queries(1, 0, "q10")
-        quantise_queries(1, 1, "q11")
         for e in range(PAGES):
-            if e > 0:
-                gather_key_scales(1, e, f"ks{e}")
             gather_key_words(1, e)
-        gather_token_scales(1, 0, 3, "row_a")
-        gather_values()
+        gather_token_scales(0, 1, 2, "max0_1")
         row_sums(0)
-        for h in range(QT):
-            for e in range(PAGES):
-                weights(0, h, e, False)
+        weights_pair(0, 0)
+        weights_pair(0, 1)
         scores(1, 0)
-        exps(1, 0)
-        finish(0, 0)
+        exps(1, 0, "p10")
+        gather_token_scales(1, 0, 3, "row_a")
+        quantise_queries(1, 1, "q11")
+        load_values()
         scores(1, 1)
-        exps(1, 1)
-        finish(0, 1)
+        exps(1, 1, "p11")
+        weights_pair(0, 2)
+        gather_values()
         row_sums(1)
-        for h in range(QT):
-            for e in range(PAGES):
-                weights(1, h, e, (h, e) != (0, 2))
-            finish(1, h)
+        for h, e in [(0,0),(0,1),(0,2),(1,0),(1,1),(1,2)]:
+            weights(1, h, e, (h, e) not in [])
+        finish(1, 0, "bank2")
+        finish(0, 0, "bank6")
+        finish(0, 1, "bank7")
+        finish(1, 1, "bank5")

from contextlib import ExitStack

import concourse.mybir as mybir
from concourse.masks import make_identity

B, N, T, D, DV, NQ = 2, 1536, 4096, 512, 128, 256
PAGE = 512
FLOPS = 2 * B * NQ * N * (D + DV)

F32 = mybir.dt.float32
BF16 = mybir.dt.bfloat16
I32 = mybir.dt.int32
U32 = mybir.dt.uint32
U16 = mybir.dt.uint16
U8 = mybir.dt.uint8
FP8X4 = mybir.dt.float8_e4m3fn_x4
ACT = mybir.ActivationFunctionType
ALU = mybir.AluOpType
AX = mybir.AxisListType

P = 128
PACK = 4
PAGES = N // PAGE
QT = NQ // P
LIST_COLS = PAGE // 16
TS_ROW = 80
SCORE_BANK = {(b, h, e): f"bank{PAGES * h + e}" for b in range(B) for h in range(QT) for e in range(PAGES)}


def tile_attend_pkv8_soft_kernel(tc, qT, k_words, k_scales, v_words, v_scales, vs, offs, voffs, out):
    nc = tc.nc
    with ExitStack() as ctx:
        lists = ctx.enter_context(tc.tile_pool(name="lists", bufs=1))
        keep = ctx.enter_context(tc.tile_pool(name="keep", bufs=1))
        ring = ctx.enter_context(tc.tile_pool(name="ring", bufs=3))
        slots = ctx.enter_context(tc.tile_pool(name="slots", bufs=1))
        ps_page = ctx.enter_context(tc.psum_pool(name="ps_page", bufs=1))

        offs_sb = lists.tile([P, B * N // 16], U16, name="offs_sb")
        voffs_sb = lists.tile([P, B * PAGES * DV // 16], U16, name="voffs_sb")

        ks_pool = keep.tile([P, T], U8, name="ks_pool", align_bytes=64)
        ts_pool = keep.tile([P, T], F32, name="ts_pool", align_bytes=64)
        ident = keep.tile([P, P], F32, name="ident", align_bytes=64)
        warm = keep.tile([P, 8], F32, name="warm")
        warm_out = keep.tile([P, 8], F32, name="warm_out")

        nc.vector.memset(ks_pool[:].bitcast(I32), 0)
        nc.vector.memset(warm[:], 0.0)
        nc.scalar.activation(warm_out[:], warm[:], ACT.Exp)
        nc.vector.memset(ts_pool[:], 0.0)
        nc.vector.memset(ident[:], 0.0)
        make_identity(nc, ident[:], nomemset=True)

        q_raw = {}

        def load_queries(b, h0, tiles, tag):
            raw = slots.tile([P, PACK, tiles * P], F32, name=f"q_raw{b}_{h0}", tag=tag, align_bytes=64)
            nc.sync.dma_start(raw[:], qT[b][:, h0 * P : (h0 + tiles) * P].rearrange("(p j) q -> p j q", j=PACK))
            for i in range(tiles):
                q_raw[b, h0 + i] = raw[:, :, i * P : (i + 1) * P]

        load_queries(0, 0, 1, "q_first")
        nc.sync.dma_start(offs_sb[:], offs)
        nc.sync.dma_start(voffs_sb[:], voffs)
        for r in range(4):
            nc.sync.dma_start(ks_pool[r:P:32, :].bitcast(I32), k_scales[0, r:16:4, :].bitcast(I32))
        kw_pool = keep.tile([P, T], I32, name="kw_pool", align_bytes=64)
        nc.sync.dma_start(kw_pool[:], k_words[0].rearrange("p n r -> p (n r)").bitcast(I32))
        load_queries(0, 1, 1, "q_second")
        load_queries(1, 0, 2, "q_third")
        nc.scalar.dma_start(ts_pool[TS_ROW : TS_ROW + 1, :], vs[TS_ROW : TS_ROW + 1, :])

        kw, ks, tsc, qw, qs = {}, {}, {}, {}, {}
        neg_max, sums, p_sb, ww, wsc, banks, inv, values = {}, {}, {}, {}, {}, {}, {}, {}

        def page_list(b, e, pages=1):
            c0 = (b * PAGES + e) * LIST_COLS
            return offs_sb[:, c0 : c0 + pages * LIST_COLS]

        def gather_key_scales(b):
            ks[b] = keep.tile([P, N], U8, name=f"ks{b}", align_bytes=64)
            nc.vector.tensor_copy(ks[b][:], ks_pool[:].indirect(page_list(b, 0, PAGES)))

        def gather_key_words(b, e):
            kw[b, e] = slots.tile([P, PAGE], U32, name=f"kw{b}_{e}", tag=f"kw{e}", align_bytes=64)
            nc.vector.tensor_copy(kw[b, e][:], kw_pool[:].bitcast(U32).indirect(page_list(b, e)))

        def gather_token_scales(b, e0, pages, tag):
            row = slots.tile([P, pages * PAGE], F32, name=f"ts_row{b}_{e0}", tag=tag, align_bytes=64)
            nc.vector.tensor_copy(row[:], ts_pool[:].indirect(page_list(b, e0, pages)))
            for i in range(pages):
                tsc[b, e0 + i] = keep.tile([P, PACK], F32, name=f"tsc{b}_{e0 + i}")
                nc.sync.dma_start(tsc[b, e0 + i][:],
                                  row[TS_ROW : TS_ROW + 1, i * PAGE : (i + 1) * PAGE].rearrange("o (s t) -> o s t", t=PACK))

        def load_values():
            vw_pool = slots.tile([P, T // PAGE * DV], I32, name="vw_pool", tag="q10", align_bytes=64)
            vsc_pool = slots.tile([P, T // PAGE * DV], U8, name="vsc_pool", tag="q11", align_bytes=64)
            nc.sync.dma_start(vw_pool[:].rearrange("p (u e) -> p u e", e=DV),
                              v_words.rearrange("u p e r -> p u (e r)").bitcast(I32))
            nc.vector.memset(vsc_pool[:].bitcast(I32), 0)
            for r in range(4):
                rows = vsc_pool[r:P:32, :].bitcast(I32)
                nc.sync.dma_start(rows.rearrange("p (u e) -> p u e", u=T // PAGE),
                                  v_scales[:, r:16:4, :].rearrange("u f e -> f u e").bitcast(I32))
            values["word_pool"], values["scale_pool"] = vw_pool, vsc_pool

        def gather_values():
            values["words"] = slots.tile([P, B * PAGES * DV], U32, name="vw", tag="vwown", align_bytes=64)
            nc.vector.tensor_copy(values["words"][:], values["word_pool"][:].bitcast(U32).indirect(voffs_sb[:]))
            values["scales"] = slots.tile([P, B * PAGES * DV], U8, name="vsc", tag="q10", align_bytes=64)
            nc.vector.tensor_copy(values["scales"][:], values["scale_pool"][:].indirect(voffs_sb[:]))

        def quantise_queries(b, h, tag):
            grouped = slots.tile([P, P, PACK], BF16, name=f"q_grouped{b}_{h}", tag=tag, align_bytes=64)
            nc.scalar.copy(grouped[:], q_raw[b, h].rearrange("p j q -> p q j"))
            qw[b, h] = slots.tile([P, P], U32, name=f"qw{b}_{h}", tag=f"qw{b}{h}", align_bytes=64)
            qs[b, h] = keep.tile([P, P], U8, name=f"qs{b}_{h}", align_bytes=64)
            nc.vector.quantize_mx(out=qw[b, h][:].bitcast(FP8X4), scales=qs[b, h][:],
                                  in_=grouped[:].rearrange("p q j -> p (q j)"))

        def scores(b, h):
            page_max = slots.tile([P, PAGES], F32, name=f"page_max{b}_{h}", tag=f"max{b}_{h}", align_bytes=64)
            for e in range(PAGES):
                bank = ps_page.tile([P, PAGE], F32, name=f"score{b}_{h}_{e}", tag=SCORE_BANK[b, h, e])
                banks[b, h, e] = bank
                nc.tensor.matmul_mx(out=bank[:], lhsT=qw[b, h][:].bitcast(FP8X4), lhsT_scale=qs[b, h][:],
                                    rhs=kw[b, e][:].bitcast(FP8X4), rhs_scale=ks[b][:, e * PAGE : (e + 1) * PAGE],
                                    start=True, stop=True)
                nc.vector.tensor_reduce(page_max[:, e : e + 1], bank[:], AX.X, ALU.max)
            neg_max[b, h] = keep.tile([P, 1], F32, name=f"neg_max{b}_{h}")
            nc.vector.tensor_reduce(neg_max[b, h][:], page_max[:], AX.X, ALU.max, negate=True)

        def exps(b, h, first_tag):
            if h == 0:
                sums[b] = keep.tile([P, QT, PAGES], F32, name=f"sums{b}")
            for e in range(PAGES):
                p_sb[b, h, e] = slots.tile([P, PACK, P], F32, name=f"p{b}_{h}_{e}", align_bytes=64,
                                           tag=first_tag if e == 0 else f"p{b}_{h}_{e}")
                nc.scalar.activation(p_sb[b, h, e][:], banks[b, h, e][:].rearrange("q (s t) -> q t s", t=PACK),
                                     ACT.Exp, bias=neg_max[b, h][:], accum_out=sums[b][:, h, e : e + 1])

        def row_sums(b):
            total = keep.tile([P, QT], F32, name=f"total{b}")
            nc.vector.tensor_reduce(total[:], sums[b][:], AX.X, ALU.add)
            inv[b] = keep.tile([P, QT], F32, name=f"inv{b}")
            nc.vector.reciprocal(inv[b][:], total[:])

        def weave(woven, planes):
            nc.scalar.copy(woven[:].rearrange("s (c i) t -> s c t i", i=4), planes[:].rearrange("s t (c i) -> s c t i", i=4))

        def weights_pair(b, e):
            planes = slots.tile([P, PACK, NQ], BF16, name=f"planes2_{e}", tag=f"planes{e}", align_bytes=64)
            for half in range(2):
                turned = ps_page.tile([P, 2, NQ], F32, name=f"turned{b}_{half}_{e}", tag=f"bank{6 + half}")
                for i in range(2):
                    for h in range(QT):
                        nc.tensor.transpose(turned[:, i, h * P : (h + 1) * P], p_sb[b, h, e][:, 2 * half + i, :], ident[:])
                for i in range(2):
                    t = 2 * half + i
                    nc.scalar.activation(planes[:, t, :], turned[:, i, :], ACT.Copy, scale=tsc[b, e][:, t : t + 1])
            woven = keep.tile([P, NQ, PACK], BF16, name=f"woven{b}_{e}", align_bytes=64)
            weave(woven, planes)
            words = keep.tile([P, NQ], U32, name=f"ww{b}_{e}", align_bytes=64)
            scales = keep.tile([P, NQ], U8, name=f"wsc{b}_{e}", align_bytes=64)
            nc.vector.quantize_mx(out=words[:].bitcast(FP8X4), scales=scales[:], in_=woven[:].rearrange("s q t -> s (q t)"))
            for h in range(QT):
                ww[b, h, e] = words[:, h * P : (h + 1) * P]
                wsc[b, h, e] = scales[:, h * P : (h + 1) * P]

        def weights(b, h, e, on_vector):
            turned = ps_page.tile([P, PACK, P], F32, name=f"turned{b}_{h}_{e}", tag=SCORE_BANK[b, h, e])
            for t in range(PACK):
                nc.tensor.transpose(turned[:, t, :], p_sb[b, h, e][:, t, :], ident[:])
            woven = keep.tile([P, P, PACK], BF16, name=f"woven{b}_{h}_{e}", align_bytes=64)
            if on_vector:
                nc.vector.tensor_tensor(woven[:], turned[:].rearrange("s t q -> s q t"),
                                        tsc[b, e][:].unsqueeze(1).to_broadcast([P, P, PACK]), ALU.mult)
            else:
                planes = ring.tile([P, PACK, P], BF16, name="planes", align_bytes=64)
                for t in range(PACK):
                    nc.scalar.activation(planes[:, t, :], turned[:, t, :], ACT.Copy, scale=tsc[b, e][:, t : t + 1])
                weave(woven, planes)
            words = keep.tile([P, P], U32, name=f"ww{b}_{h}_{e}", align_bytes=64)
            scales = keep.tile([P, P], U8, name=f"wsc{b}_{h}_{e}", align_bytes=64)
            nc.vector.quantize_mx(out=words[:].bitcast(FP8X4), scales=scales[:], in_=woven[:].rearrange("s q t -> s (q t)"))
            ww[b, h, e], wsc[b, h, e] = words[:], scales[:]

        def finish(b, h, tag):
            acc = ps_page.tile([P, DV], F32, name=f"acc{b}_{h}", tag=tag)
            for e in range(PAGES):
                cols = slice((b * PAGES + e) * DV, (b * PAGES + e + 1) * DV)
                nc.tensor.matmul_mx(out=acc[:], lhsT=ww[b, h, e].bitcast(FP8X4), lhsT_scale=wsc[b, h, e],
                                    rhs=values["words"][:, cols].bitcast(FP8X4), rhs_scale=values["scales"][:, cols],
                                    start=(e == 0), stop=(e == PAGES - 1))
            y = keep.tile([P, DV], F32, name=f"y{b}_{h}")
            nc.scalar.activation(y[:], acc[:], ACT.Copy, scale=inv[b][:, h : h + 1])
            nc.sync.dma_start(out[b, h * P : (h + 1) * P, :], y[:])

        quantise_queries(0, 0, "q00")
        gather_key_scales(0)
        gather_key_scales(1)
        for e in range(PAGES):
            gather_key_words(0, e)
        scores(0, 0)
        quantise_queries(0, 1, "row_a")
        gather_token_scales(0, 0, 1, "row_a")
        scores(0, 1)
        exps(0, 0, "p00")
        exps(0, 1, "p01")
        quantise_queries(1, 0, "q10")
        for e in range(PAGES):
            gather_key_words(1, e)
        gather_token_scales(0, 1, 2, "max0_1")
        row_sums(0)
        weights_pair(0, 0)
        weights_pair(0, 1)
        scores(1, 0)
        exps(1, 0, "p10")
        gather_token_scales(1, 0, 3, "row_a")
        quantise_queries(1, 1, "q11")
        load_values()
        scores(1, 1)
        exps(1, 1, "p11")
        weights_pair(0, 2)
        gather_values()
        row_sums(1)
        for h, e in [(0,0),(0,1),(0,2),(1,0),(1,1),(1,2)]:
            weights(1, h, e, (h, e) not in [])
        finish(1, 0, "bank2")
        finish(0, 0, "bank6")
        finish(0, 1, "bank7")
        finish(1, 1, "bank5")
